import numpy as np
import ml_dtypes


def mxq(x, axis, fmt="e4m3"):
    dtype, down = {"e4m3": (ml_dtypes.float8_e4m3fn, 7), "e5m2": (ml_dtypes.float8_e5m2, 14)}[fmt]
    v = np.moveaxis(np.asarray(x, np.float32).astype(ml_dtypes.bfloat16).astype(np.float64), axis, -1)
    blocks = v.reshape(v.shape[:-1] + (-1, 32))
    amax = np.abs(blocks).max(-1, keepdims=True)
    byte = np.maximum(np.where(amax > 0, np.frexp(amax)[1] - 1 + 127, 0) - down, 1)
    scale = np.exp2(byte - 127.0)
    codes = (blocks / scale).astype(np.float32).astype(dtype).astype(np.float64)
    return np.moveaxis((codes * scale).reshape(v.shape), -1, axis)


WIDE = False


def mx_kscale(k):
    if not WIDE:
        return np.ones(k)
    levels = np.array([30, -30])
    if k % 512:
        return np.exp2(np.random.permutation(np.resize(levels, k // 32))).repeat(32)
    a = np.empty((k // 512, 16))
    for p in range(k // 512):
        a[p, :8] = np.random.permutation(np.resize(levels, 8))
        for g in range(8):
            far = levels[np.abs(levels - a[p, g]) >= 10]
            a[p, g + 8] = far[np.random.randint(len(far))]
    return np.exp2(a.ravel()).repeat(32)


def f64(x):
    return np.asarray(x).astype(np.float64)


def striped(idx):
    return np.tile(np.asarray(idx).reshape(-1, 16).T, (8, 1)).astype(np.uint16)


def unstriped(offs):
    return offs[:16].T.reshape(-1).astype(np.int64)


E2M1 = np.array([0.0, 0.5, 1.0, 1.5, 2.0, 3.0, 4.0, 6.0, -0.0, -0.5, -1.0, -1.5, -2.0, -3.0, -4.0, -6.0])


def pack_weight(w, fmt):
    k, n = w.shape
    w = f64(np.asarray(w, np.float32).astype(ml_dtypes.bfloat16)).reshape(k // 32, 32, n)
    amax = np.abs(w).max(1)
    if fmt == "e4m3":
        byte = np.frexp(amax)[1] - 1 + 127 - 7
    else:
        mant, ex = np.frexp(amax / 6.0)
        byte = np.where(mant > 0.5, ex, ex - 1) + 127
    byte = np.clip(np.where(amax > 0, byte, 1), 1, 254)
    scaled = (w * np.exp2(127.0 - byte)[:, None, :]).reshape(k, n).astype(np.float32)
    by_word = np.ascontiguousarray(scaled.reshape(k // 512, 128, 4, n).transpose(0, 1, 3, 2))
    if fmt == "e4m3":
        words = by_word.astype(ml_dtypes.float8_e4m3fn).view(np.uint8)
    else:
        c = by_word.astype(ml_dtypes.float4_e2m1fn).view(np.uint8) & 0xF
        words = (c[..., 0::2] | (c[..., 1::2] << 4)).reshape(k // 512, 128, 2 * n)
    return np.ascontiguousarray(words), np.ascontiguousarray(byte.astype(np.uint8).reshape(k // 512, 16, n))


def unpack_weight(words, scales, fmt):
    g, _, n = scales.shape
    words = np.ascontiguousarray(words).reshape(g, 128, n, -1)
    if fmt == "e4m3":
        vals = words.view(ml_dtypes.float8_e4m3fn).astype(np.float64)
    else:
        nib = np.empty((g, 128, n, 4), np.uint8)
        nib[..., 0::2] = words & 0xF
        nib[..., 1::2] = words >> 4
        vals = E2M1[nib]
    vals = vals * np.repeat(np.exp2(scales.astype(np.float64) - 127.0), 8, axis=1)[..., None]
    return vals.transpose(0, 1, 3, 2).reshape(g * 512, n)


K, T, J, I, V = 1024, 1024, 256, 256, 1024


def setup_inputs():
    n = np.random.standard_normal
    idx = np.random.permutation(T)[:J]
    idx2 = np.random.permutation(V)[:I]
    fk = mx_kscale(K)
    xtp = pack_weight(n((K, T)) * 0.04 * fk[:, None], "e2m1")
    return {
        "xt_words": xtp[0],
        "xt_scales": xtp[1],
        "ky": (n((K, V)) / fk[:, None]).astype(np.float32),
        "bi": (np.random.uniform(-0.7, 0.7, (1, I))).astype(np.float32),
        "pr": (np.random.uniform(0.5, 1.5, (1, I))).astype(np.float32),
        "offs": striped(idx),
        "offs2": striped(idx2),
    }


def reference(xt_words, xt_scales, ky, bi, pr, offs, offs2):
    idx = unstriped(offs)
    idx2 = unstriped(offs2)
    xtu = unpack_weight(xt_words, xt_scales, "e2m1")
    xtidxg = xtu[:, idx]
    kyidx2q = mxq(f64(ky)[:, idx2], 0, "e5m2")
    a0 = xtidxg.T @ kyidx2q
    a = a0 + f64(bi)
    e = np.exp(0.7 * a) * f64(pr)
    y = 256.0 * e / np.sum(e, axis=1, keepdims=True) - f64(pr)
    return y

@@ -1,0 +1,168 @@
+from contextlib import ExitStack
+
+import concourse.mybir as mybir
+from concourse.masks import make_identity
+
+K, T, J, I, V = 1024, 1024, 256, 256, 1024
+FLOPS = 2 * K * J * I
+
+F32 = mybir.dt.float32
+BF16 = mybir.dt.bfloat16
+I32 = mybir.dt.int32
+U32 = mybir.dt.uint32
+U16 = mybir.dt.uint16
+U8 = mybir.dt.uint8
+E2M1 = mybir.dt.float4_e2m1fn_x4
+E5M2 = mybir.dt.float8_e5m2_x4
+ALU = mybir.AluOpType
+ACT = mybir.ActivationFunctionType
+
+P = 128
+PACK = 4
+PASSES = K // (P * PACK)
+HALVES = J // P
+LIST_COLS = P // 16
+TEMP = 0.7
+SHARE = 256.0
+
+
+def tile_list_scores_picked_listed_shares_kernel(tc, xt_words, xt_scales, ky, bi, pr, offs, offs2, out):
+    nc = tc.nc
+    with ExitStack() as ctx:
+        lists = ctx.enter_context(tc.tile_pool(name="lists", bufs=1))
+        sb = ctx.enter_context(tc.tile_pool(name="sb", bufs=1))
+        ps = ctx.enter_context(tc.psum_pool(name="ps", bufs=1))
+
+        tok_list = lists.tile([P, J // 16], U16, name="tok_list")
+        key_list = lists.tile([P, I // 16], U16, name="key_list")
+        planes = [[sb.tile([P, V], F32, name=f"plane{z}{t}") for t in range(PACK)] for z in range(PASSES)]
+        words = [sb.tile([P, T], U16, name=f"words{z}") for z in range(PASSES)]
+        scale_rows = sb.tile([P, PASSES, T], U8, name="scale_rows")
+        ky_rows = ky.rearrange("(z p t) v -> z t p v", z=PASSES, t=PACK)
+
+        def load_plane(z, t):
+            nc.sync.dma_start(out=planes[z][t][:], in_=ky_rows[z, t])
+
+        def load_words(z):
+            nc.sync.dma_start(out=words[z][:].bitcast(I32), in_=xt_words[z].bitcast(I32))
+
+        load_plane(0, 0)
+        nc.sync.dma_start(key_list[:], offs2)
+        load_plane(0, 1)
+        nc.sync.dma_start(tok_list[:], offs)
+        load_plane(0, 2)
+        load_plane(0, 3)
+        load_words(0)
+        for t in range(PACK):
+            load_plane(1, t)
+        load_words(1)
+
+        scale_i32 = scale_rows[:].rearrange("p z c -> p (z c)").bitcast(I32)
+        nc.vector.memset(scale_i32, 0)
+        src_scales = xt_scales.bitcast(I32).rearrange("z q c -> q z c")
+        dst_scales = scale_i32.rearrange("p (z c) -> p z c", z=PASSES)
+        for q in range(4):
+            nc.scalar.dma_start(out=dst_scales[32 * q : 32 * q + 4], in_=src_scales[4 * q : 4 * q + 4])
+        bi_col = sb.tile([P, 2], F32, name="bi_col")
+        pr_col = sb.tile([P, 2], F32, name="pr_col")
+        nc.scalar.dma_start(out=bi_col[:], in_=bi.rearrange("o (p c) -> (o p) c", c=2))
+        nc.scalar.dma_start(out=pr_col[:], in_=pr.rearrange("o (p c) -> (o p) c", c=2))
+        ident = sb.tile([P, P], F32, name="ident")
+        make_identity(nc, ident[:])
+
+        spread = ps.tile([P, 4, P], F32, name="spread")
+        for c in range(2):
+            nc.tensor.transpose(spread[:, c, :], bi_col[:, c : c + 1].to_broadcast([P, P]), ident[:])
+        for c in range(2):
+            nc.tensor.transpose(spread[:, 2 + c, :], pr_col[:, c : c + 1].to_broadcast([P, P]), ident[:])
+
+        picked = sb.tile([P, PACK, I], BF16, name="picked")
+        for t in range(PACK):
+            nc.scalar.activation(picked[:, t, :], planes[0][t][:].indirect(key_list[:]), ACT.Copy)
+        neg_bias = sb.tile([P, I], F32, name="neg_bias")
+        prior = sb.tile([P, I], F32, name="prior")
+        nc.scalar.activation(
+            neg_bias[:].rearrange("p (n c) -> p n c", c=2),
+            spread[:, 0:2, :].rearrange("p c n -> p n c"),
+            ACT.Copy,
+            scale=-TEMP,
+        )
+        nc.scalar.copy(prior[:].rearrange("p (n c) -> p n c", c=2), spread[:, 2:4, :].rearrange("p c n -> p n c"))
+
+        tok_scales = [sb.tile([P, J], U8, name=f"tok_scales{z}", align_bytes=64) for z in range(PASSES)]
+        for z in range(PASSES):
+            nc.vector.tensor_copy(tok_scales[z][:], scale_rows[:, z, :].indirect(tok_list[:]))
+
+        grouped = [sb.tile([P, I, PACK], BF16, name=f"grouped{z}", align_bytes=64) for z in range(PASSES)]
+        key_codes = [sb.tile([P, I], U32, name=f"key_codes{z}", align_bytes=64) for z in range(PASSES)]
+        key_scales = [sb.tile([P, I], U8, name=f"key_scales{z}", align_bytes=64) for z in range(PASSES)]
+        tok_words = [
+            [sb.tile([P, P], U16, name=f"tok_words{z}{h}", align_bytes=64) for h in range(HALVES)]
+            for z in range(PASSES)
+        ]
+        acc = [ps.tile([P, I], F32, name=f"acc{h}") for h in range(HALVES)]
+
+        def quantize(z):
+            nc.vector.quantize_mx(
+                out=key_codes[z][:].bitcast(E5M2),
+                scales=key_scales[z][:],
+                in_=grouped[z][:].rearrange("p i t -> p (i t)"),
+            )
+
+        def pick_words(z, h):
+            nc.vector.tensor_copy(
+                tok_words[z][h][:], words[z][:].indirect(tok_list[:, LIST_COLS * h : LIST_COLS * (h + 1)])
+            )
+
+        def multiply(z, h):
+            nc.tensor.matmul_mx(
+                out=acc[h][:],
+                lhsT=tok_words[z][h][:].bitcast(E2M1),
+                lhsT_scale=tok_scales[z][:, P * h : P * (h + 1)],
+                rhs=key_codes[z][:].bitcast(E5M2),
+                rhs_scale=key_scales[z][:],
+                start=(z == 0),
+                stop=(z == PASSES - 1),
+            )
+
+        nc.vector.tensor_copy(grouped[0][:], picked[:].rearrange("p t i -> p i t"))
+        pick_words(0, 0)
+        quantize(0)
+        pick_words(0, 1)
+        for h in range(HALVES):
+            multiply(0, h)
+
+        for t in range(PACK):
+            nc.vector.tensor_copy(grouped[1][:, :, t], planes[1][t][:].indirect(key_list[:]))
+        pick_words(1, 0)
+        quantize(1)
+        multiply(1, 0)
+        pick_words(1, 1)
+        multiply(1, 1)
+
+        neg = [sb.tile([P, I], F32, name=f"neg{h}") for h in range(HALVES)]
+        low = [sb.tile([P, 1], F32, name=f"low{h}") for h in range(HALVES)]
+        expo = [sb.tile([P, I], F32, name=f"expo{h}") for h in range(HALVES)]
+        weighted = [sb.tile([P, I], F32, name=f"weighted{h}") for h in range(HALVES)]
+        total = [sb.tile([P, 1], F32, name=f"total{h}") for h in range(HALVES)]
+        part = [sb.tile([P, 1], F32, name=f"part{h}") for h in range(HALVES)]
+        factor = [sb.tile([P, 1], F32, name=f"factor{h}") for h in range(HALVES)]
+        result = [sb.tile([P, I], F32, name=f"result{h}") for h in range(HALVES)]
+        for h in range(HALVES):
+            nc.vector.scalar_tensor_tensor(neg[h][:], acc[h][:], -TEMP, neg_bias[:], ALU.mult, ALU.add)
+        for h in range(HALVES):
+            nc.vector.tensor_reduce(low[h][:], neg[h][:], mybir.AxisListType.X, ALU.min)
+            nc.scalar.activation(expo[h][:], neg[h][:], ACT.Exp, bias=low[h][:], scale=-1.0)
+        for h in range(HALVES):
+            nc.vector.scalar_tensor_tensor(
+                weighted[h][:], expo[h][:], 1.0, prior[:], ALU.mult, ALU.mult, accum_out=total[h][:]
+            )
+        for h in range(HALVES):
+            nc.vector.tensor_scalar(part[h][:], total[h][:], 1.0 / SHARE, None, ALU.mult)
+        for h in range(HALVES):
+            nc.vector.reciprocal(factor[h][:], part[h][:])
+        for h in range(HALVES):
+            nc.vector.scalar_tensor_tensor(
+                result[h][:], weighted[h][:], factor[h][:], prior[:], ALU.mult, ALU.subtract
+            )
+            nc.sync.dma_start(out=out[P * h : P * (h + 1), :], in_=result[h][:])

@@ -57,43 +57,43 @@ def tile_list_scores_picked_listed_shares_kernel(tc, xt_words, xt_scales, ky, bi
             load_plane(1, t)
         load_words(1)
 
+        ident = sb.tile([P, P], F32, name="ident")
+        make_identity(nc, ident[:])
         scale_i32 = scale_rows[:].rearrange("p z c -> p (z c)").bitcast(I32)
         nc.vector.memset(scale_i32, 0)
         src_scales = xt_scales.bitcast(I32).rearrange("z q c -> q z c")
         dst_scales = scale_i32.rearrange("p (z c) -> p z c", z=PASSES)
         for q in range(4):
-            nc.scalar.dma_start(out=dst_scales[32 * q : 32 * q + 4], in_=src_scales[4 * q : 4 * q + 4])
-        bi_col = sb.tile([P, 2], F32, name="bi_col")
-        pr_col = sb.tile([P, 2], F32, name="pr_col")
-        nc.scalar.dma_start(out=bi_col[:], in_=bi.rearrange("o (p c) -> (o p) c", c=2))
-        nc.scalar.dma_start(out=pr_col[:], in_=pr.rearrange("o (p c) -> (o p) c", c=2))
-        ident = sb.tile([P, P], F32, name="ident")
-        make_identity(nc, ident[:])
+            nc.gpsimd.dma_start(out=dst_scales[32 * q : 32 * q + 4], in_=src_scales[4 * q : 4 * q + 4])
+        rows = sb.tile([P, 2 * I], F32, name="rows")
+        nc.vector.memset(rows[:], 0.0)
+        nc.scalar.dma_start(out=rows[0:1, 0:I], in_=bi)
+        nc.scalar.dma_start(out=rows[0:1, I : 2 * I], in_=pr)
 
+        turned = ps.tile([P, 4, P], F32, name="turned")
+        for c in range(4):
+            nc.tensor.transpose(turned[:, c, :], rows[:, P * c : P * (c + 1)], ident[:])
+        cols = sb.tile([P, 4], F32, name="cols")
+        nc.scalar.copy(cols[:], turned[:, :, 0])
         spread = ps.tile([P, 4, P], F32, name="spread")
-        for c in range(2):
-            nc.tensor.transpose(spread[:, c, :], bi_col[:, c : c + 1].to_broadcast([P, P]), ident[:])
-        for c in range(2):
-            nc.tensor.transpose(spread[:, 2 + c, :], pr_col[:, c : c + 1].to_broadcast([P, P]), ident[:])
+        for c in range(4):
+            nc.tensor.transpose(spread[:, c, :], cols[:, c : c + 1].to_broadcast([P, P]), ident[:])
+        spread_flat = spread[:].rearrange("p c n -> p (c n)")
 
         picked = sb.tile([P, PACK, I], BF16, name="picked")
         for t in range(PACK):
             nc.scalar.activation(picked[:, t, :], planes[0][t][:].indirect(key_list[:]), ACT.Copy)
+        grouped = [sb.tile([P, I, PACK], BF16, name=f"grouped{z}", align_bytes=64) for z in range(PASSES)]
+        nc.scalar.copy(grouped[0][:], picked[:].rearrange("p t i -> p i t"))
         neg_bias = sb.tile([P, I], F32, name="neg_bias")
         prior = sb.tile([P, I], F32, name="prior")
-        nc.scalar.activation(
-            neg_bias[:].rearrange("p (n c) -> p n c", c=2),
-            spread[:, 0:2, :].rearrange("p c n -> p n c"),
-            ACT.Copy,
-            scale=-TEMP,
-        )
-        nc.scalar.copy(prior[:].rearrange("p (n c) -> p n c", c=2), spread[:, 2:4, :].rearrange("p c n -> p n c"))
+        nc.scalar.activation(neg_bias[:], spread_flat[:, 0:I], ACT.Copy, scale=-TEMP)
+        nc.scalar.copy(prior[:], spread_flat[:, I : 2 * I])
 
         tok_scales = [sb.tile([P, J], U8, name=f"tok_scales{z}", align_bytes=64) for z in range(PASSES)]
         for z in range(PASSES):
             nc.vector.tensor_copy(tok_scales[z][:], scale_rows[:, z, :].indirect(tok_list[:]))
 
-        grouped = [sb.tile([P, I, PACK], BF16, name=f"grouped{z}", align_bytes=64) for z in range(PASSES)]
         key_codes = [sb.tile([P, I], U32, name=f"key_codes{z}", align_bytes=64) for z in range(PASSES)]
         key_scales = [sb.tile([P, I], U8, name=f"key_scales{z}", align_bytes=64) for z in range(PASSES)]
         tok_words = [
@@ -102,11 +102,11 @@ def tile_list_scores_picked_listed_shares_kernel(tc, xt_words, xt_scales, ky, bi
         ]
         acc = [ps.tile([P, I], F32, name=f"acc{h}") for h in range(HALVES)]
 
-        def quantize(z):
+        def quantize(z, lo, hi):
             nc.vector.quantize_mx(
-                out=key_codes[z][:].bitcast(E5M2),
-                scales=key_scales[z][:],
-                in_=grouped[z][:].rearrange("p i t -> p (i t)"),
+                out=key_codes[z][:, lo:hi].bitcast(E5M2),
+                scales=key_scales[z][:, lo:hi],
+                in_=grouped[z][:, lo:hi, :].rearrange("p i t -> p (i t)"),
             )
 
         def pick_words(z, h):
@@ -125,17 +125,22 @@ def tile_list_scores_picked_listed_shares_kernel(tc, xt_words, xt_scales, ky, bi
                 stop=(z == PASSES - 1),
             )
 
-        nc.vector.tensor_copy(grouped[0][:], picked[:].rearrange("p t i -> p i t"))
         pick_words(0, 0)
-        quantize(0)
+        quantize(0, 0, I)
         pick_words(0, 1)
         for h in range(HALVES):
             multiply(0, h)
 
-        for t in range(PACK):
+        for t in range(PACK - 1):
             nc.vector.tensor_copy(grouped[1][:, :, t], planes[1][t][:].indirect(key_list[:]))
+        for u in range(2):
+            nc.vector.tensor_copy(
+                grouped[1][:, P * u : P * (u + 1), PACK - 1],
+                planes[1][PACK - 1][:].indirect(key_list[:, LIST_COLS * u : LIST_COLS * (u + 1)]),
+            )
+        quantize(1, 0, P)
         pick_words(1, 0)
-        quantize(1)
+        quantize(1, P, I)
         multiply(1, 0)
         pick_words(1, 1)
         multiply(1, 1)
@@ -145,7 +150,7 @@ def tile_list_scores_picked_listed_shares_kernel(tc, xt_words, xt_scales, ky, bi
         expo = [sb.tile([P, I], F32, name=f"expo{h}") for h in range(HALVES)]
         weighted = [sb.tile([P, I], F32, name=f"weighted{h}") for h in range(HALVES)]
         total = [sb.tile([P, 1], F32, name=f"total{h}") for h in range(HALVES)]
-        part = [sb.tile([P, 1], F32, name=f"part{h}") for h in range(HALVES)]
+        raised = [sb.tile([P, I], F32, name=f"raised{h}") for h in range(HALVES)]
         factor = [sb.tile([P, 1], F32, name=f"factor{h}") for h in range(HALVES)]
         result = [sb.tile([P, I], F32, name=f"result{h}") for h in range(HALVES)]
         for h in range(HALVES):
@@ -158,11 +163,10 @@ def tile_list_scores_picked_listed_shares_kernel(tc, xt_words, xt_scales, ky, bi
                 weighted[h][:], expo[h][:], 1.0, prior[:], ALU.mult, ALU.mult, accum_out=total[h][:]
             )
         for h in range(HALVES):
-            nc.vector.tensor_scalar(part[h][:], total[h][:], 1.0 / SHARE, None, ALU.mult)
-        for h in range(HALVES):
-            nc.vector.reciprocal(factor[h][:], part[h][:])
+            nc.scalar.activation(raised[h][:], weighted[h][:], ACT.Copy, scale=SHARE)
+            nc.vector.reciprocal(factor[h][:], total[h][:])
         for h in range(HALVES):
             nc.vector.scalar_tensor_tensor(
-                result[h][:], weighted[h][:], factor[h][:], prior[:], ALU.mult, ALU.subtract
+                result[h][:], raised[h][:], factor[h][:], prior[:], ALU.mult, ALU.subtract
             )
             nc.sync.dma_start(out=out[P * h : P * (h + 1), :], in_=result[h][:])

@@ -38,61 +38,70 @@ def tile_list_scores_picked_listed_shares_kernel(tc, xt_words, xt_scales, ky, bi
         planes = [[sb.tile([P, V], F32, name=f"plane{z}{t}") for t in range(PACK)] for z in range(PASSES)]
         words = [sb.tile([P, T], U16, name=f"words{z}") for z in range(PASSES)]
         scale_rows = sb.tile([P, PASSES, T], U8, name="scale_rows")
-        ky_rows = ky.rearrange("(z p t) v -> z t p v", z=PASSES, t=PACK)
+        ky_rows = ky.rearrange("(z p t) v -> z p t v", z=PASSES, t=PACK)
 
         def load_plane(z, t):
-            nc.sync.dma_start(out=planes[z][t][:], in_=ky_rows[z, t])
+            nc.sync.dma_start(out=planes[z][t][:], in_=ky_rows[z, :, t, :])
 
         def load_words(z):
             nc.sync.dma_start(out=words[z][:].bitcast(I32), in_=xt_words[z].bitcast(I32))
 
-        load_plane(0, 0)
-        nc.sync.dma_start(key_list[:], offs2)
-        load_plane(0, 1)
-        nc.sync.dma_start(tok_list[:], offs)
-        load_plane(0, 2)
-        load_plane(0, 3)
-        load_words(0)
-        for t in range(PACK):
-            load_plane(1, t)
-        load_words(1)
-
-        ident = sb.tile([P, P], F32, name="ident")
-        make_identity(nc, ident[:])
         scale_i32 = scale_rows[:].rearrange("p z c -> p (z c)").bitcast(I32)
         nc.vector.memset(scale_i32, 0)
         src_scales = xt_scales.bitcast(I32).rearrange("z q c -> q z c")
         dst_scales = scale_i32.rearrange("p (z c) -> p z c", z=PASSES)
-        for q in range(4):
-            nc.gpsimd.dma_start(out=dst_scales[32 * q : 32 * q + 4], in_=src_scales[4 * q : 4 * q + 4])
-        rows = sb.tile([P, 2 * I], F32, name="rows")
-        nc.vector.memset(rows[:], 0.0)
-        nc.scalar.dma_start(out=rows[0:1, 0:I], in_=bi)
-        nc.scalar.dma_start(out=rows[0:1, I : 2 * I], in_=pr)
+        ident = sb.tile([P, P], F32, name="ident")
+        make_identity(nc, ident[:])
 
-        turned = ps.tile([P, 4, P], F32, name="turned")
-        for c in range(4):
-            nc.tensor.transpose(turned[:, c, :], rows[:, P * c : P * (c + 1)], ident[:])
-        cols = sb.tile([P, 4], F32, name="cols")
-        nc.scalar.copy(cols[:], turned[:, :, 0])
+        bi_col = sb.tile([P, 2], F32, name="bi_col")
+        pr_col = sb.tile([P, 2], F32, name="pr_col")
+        load_plane(0, 0)
+        nc.sync.dma_start(key_list[:], offs2)
+        nc.sync.dma_start(tok_list[:], offs)
+        nc.sync.dma_start(out=bi_col[:], in_=bi.rearrange("o (p c) -> (o p) c", c=2))
+        nc.sync.dma_start(out=pr_col[:], in_=pr.rearrange("o (p c) -> (o p) c", c=2))
+        load_words(0)
+        load_plane(0, 1)
+        load_plane(0, 2)
+        nc.sync.dma_start(out=dst_scales[0:P:8], in_=src_scales)
+        load_plane(0, 3)
+        for t in range(PACK):
+            load_plane(1, t)
+        load_words(1)
+
         spread = ps.tile([P, 4, P], F32, name="spread")
-        for c in range(4):
-            nc.tensor.transpose(spread[:, c, :], cols[:, c : c + 1].to_broadcast([P, P]), ident[:])
-        spread_flat = spread[:].rearrange("p c n -> p (c n)")
+        for c in range(2):
+            nc.tensor.transpose(spread[:, c, :], bi_col[:, c : c + 1].to_broadcast([P, P]), ident[:])
+        for c in range(2):
+            nc.tensor.transpose(spread[:, 2 + c, :], pr_col[:, c : c + 1].to_broadcast([P, P]), ident[:])
 
         picked = sb.tile([P, PACK, I], BF16, name="picked")
+        picked_late = sb.tile([P, 2, I], BF16, name="picked_late")
         for t in range(PACK):
             nc.scalar.activation(picked[:, t, :], planes[0][t][:].indirect(key_list[:]), ACT.Copy)
         grouped = [sb.tile([P, I, PACK], BF16, name=f"grouped{z}", align_bytes=64) for z in range(PASSES)]
-        nc.scalar.copy(grouped[0][:], picked[:].rearrange("p t i -> p i t"))
         neg_bias = sb.tile([P, I], F32, name="neg_bias")
         prior = sb.tile([P, I], F32, name="prior")
-        nc.scalar.activation(neg_bias[:], spread_flat[:, 0:I], ACT.Copy, scale=-TEMP)
-        nc.scalar.copy(prior[:], spread_flat[:, I : 2 * I])
+        nc.scalar.activation(
+            neg_bias[:].rearrange("p (n c) -> p n c", c=2),
+            spread[:, 0:2, :].rearrange("p c n -> p n c"),
+            ACT.Copy,
+            scale=-TEMP,
+        )
+        nc.scalar.copy(prior[:].rearrange("p (n c) -> p n c", c=2), spread[:, 2:4, :].rearrange("p c n -> p n c"))
 
-        tok_scales = [sb.tile([P, J], U8, name=f"tok_scales{z}", align_bytes=64) for z in range(PASSES)]
+        for t in range(2):
+            nc.scalar.activation(picked_late[:, t, :], planes[1][t][:].indirect(key_list[:]), ACT.Copy)
+
+        picked_scales = sb.tile([P, PASSES, J], U8, name="picked_scales")
+        tok_scales = sb.tile([P, PASSES, J], U8, name="tok_scales", align_bytes=64)
+        tok_scales_i32 = tok_scales[:].rearrange("p z j -> p (z j)").bitcast(I32)
+        picked_scales_i32 = picked_scales[:].rearrange("p z j -> p (z j)").bitcast(I32)
+        nc.vector.memset(tok_scales_i32, 0)
         for z in range(PASSES):
-            nc.vector.tensor_copy(tok_scales[z][:], scale_rows[:, z, :].indirect(tok_list[:]))
+            nc.vector.tensor_copy(picked_scales[:, z, :], scale_rows[:, z, :].indirect(tok_list[:]))
+        for r in range(4):
+            nc.scalar.dma_start(out=tok_scales_i32[r:P:32], in_=picked_scales_i32[8 * r : P : 32])
 
         key_codes = [sb.tile([P, I], U32, name=f"key_codes{z}", align_bytes=64) for z in range(PASSES)]
         key_scales = [sb.tile([P, I], U8, name=f"key_scales{z}", align_bytes=64) for z in range(PASSES)]
@@ -118,7 +127,7 @@ def tile_list_scores_picked_listed_shares_kernel(tc, xt_words, xt_scales, ky, bi
             nc.tensor.matmul_mx(
                 out=acc[h][:],
                 lhsT=tok_words[z][h][:].bitcast(E2M1),
-                lhsT_scale=tok_scales[z][:, P * h : P * (h + 1)],
+                lhsT_scale=tok_scales[:, z, P * h : P * (h + 1)],
                 rhs=key_codes[z][:].bitcast(E5M2),
                 rhs_scale=key_scales[z][:],
                 start=(z == 0),
@@ -126,18 +135,18 @@ def tile_list_scores_picked_listed_shares_kernel(tc, xt_words, xt_scales, ky, bi
             )
 
         pick_words(0, 0)
-        quantize(0, 0, I)
         pick_words(0, 1)
+        nc.vector.tensor_copy(grouped[0][:], picked[:].rearrange("p t i -> p i t"))
+        quantize(0, 0, I)
         for h in range(HALVES):
             multiply(0, h)
 
-        for t in range(PACK - 1):
-            nc.vector.tensor_copy(grouped[1][:, :, t], planes[1][t][:].indirect(key_list[:]))
-        for u in range(2):
-            nc.vector.tensor_copy(
-                grouped[1][:, P * u : P * (u + 1), PACK - 1],
-                planes[1][PACK - 1][:].indirect(key_list[:, LIST_COLS * u : LIST_COLS * (u + 1)]),
-            )
+        nc.vector.tensor_copy(grouped[1][:, :, 0:2], picked_late[:].rearrange("p t i -> p i t"))
+        nc.vector.tensor_copy(grouped[1][:, :, 2], planes[1][2][:].indirect(key_list[:]))
+        picked_last = sb.tile([P, P], BF16, name="picked_last")
+        nc.scalar.activation(picked_last[:], planes[1][3][:].indirect(key_list[:, LIST_COLS:]), ACT.Copy)
+        nc.vector.tensor_copy(grouped[1][:, 0:P, 3], planes[1][3][:].indirect(key_list[:, 0:LIST_COLS]))
+        nc.vector.tensor_copy(grouped[1][:, P:I, 3], picked_last[:])
         quantize(1, 0, P)
         pick_words(1, 0)
         quantize(1, P, I)

from contextlib import ExitStack

import concourse.mybir as mybir
from concourse.masks import make_identity

K, T, J, I, V = 1024, 1024, 256, 256, 1024
FLOPS = 2 * K * J * I

F32 = mybir.dt.float32
BF16 = mybir.dt.bfloat16
I32 = mybir.dt.int32
U32 = mybir.dt.uint32
U16 = mybir.dt.uint16
U8 = mybir.dt.uint8
E2M1 = mybir.dt.float4_e2m1fn_x4
E5M2 = mybir.dt.float8_e5m2_x4
ALU = mybir.AluOpType
ACT = mybir.ActivationFunctionType

P = 128
PACK = 4
PASSES = K // (P * PACK)
HALVES = J // P
LIST_COLS = P // 16
TEMP = 0.7
SHARE = 256.0


def tile_list_scores_picked_listed_shares_kernel(tc, xt_words, xt_scales, ky, bi, pr, offs, offs2, out):
    nc = tc.nc
    with ExitStack() as ctx:
        lists = ctx.enter_context(tc.tile_pool(name="lists", bufs=1))
        sb = ctx.enter_context(tc.tile_pool(name="sb", bufs=1))
        ps = ctx.enter_context(tc.psum_pool(name="ps", bufs=1))

        tok_list = lists.tile([P, J // 16], U16, name="tok_list")
        key_list = lists.tile([P, I // 16], U16, name="key_list")
        planes = [[sb.tile([P, V], F32, name=f"plane{z}{t}") for t in range(PACK)] for z in range(PASSES)]
        words = [sb.tile([P, T], U16, name=f"words{z}") for z in range(PASSES)]
        scale_rows = sb.tile([P, PASSES, T], U8, name="scale_rows")
        ky_rows = ky.rearrange("(z p t) v -> z p t v", z=PASSES, t=PACK)

        def load_plane(z, t):
            nc.sync.dma_start(out=planes[z][t][:], in_=ky_rows[z, :, t, :])

        def load_words(z):
            nc.sync.dma_start(out=words[z][:].bitcast(I32), in_=xt_words[z].bitcast(I32))

        scale_i32 = scale_rows[:].rearrange("p z c -> p (z c)").bitcast(I32)
        nc.vector.memset(scale_i32, 0)
        src_scales = xt_scales.bitcast(I32).rearrange("z q c -> q z c")
        dst_scales = scale_i32.rearrange("p (z c) -> p z c", z=PASSES)
        ident = sb.tile([P, P], F32, name="ident")
        make_identity(nc, ident[:])

        bi_col = sb.tile([P, 2], F32, name="bi_col")
        pr_col = sb.tile([P, 2], F32, name="pr_col")
        load_plane(0, 0)
        nc.sync.dma_start(key_list[:], offs2)
        nc.sync.dma_start(tok_list[:], offs)
        nc.sync.dma_start(out=bi_col[:], in_=bi.rearrange("o (p c) -> (o p) c", c=2))
        nc.sync.dma_start(out=pr_col[:], in_=pr.rearrange("o (p c) -> (o p) c", c=2))
        load_words(0)
        load_plane(0, 1)
        load_plane(0, 2)
        nc.sync.dma_start(out=dst_scales[0:P:8], in_=src_scales)
        load_plane(0, 3)
        for t in range(PACK):
            load_plane(1, t)
        load_words(1)

        spread = ps.tile([P, 4, P], F32, name="spread")
        for c in range(2):
            nc.tensor.transpose(spread[:, c, :], bi_col[:, c : c + 1].to_broadcast([P, P]), ident[:])
        for c in range(2):
            nc.tensor.transpose(spread[:, 2 + c, :], pr_col[:, c : c + 1].to_broadcast([P, P]), ident[:])

        picked = sb.tile([P, PACK, I], BF16, name="picked")
        picked_late = sb.tile([P, 2, I], BF16, name="picked_late")
        for t in range(PACK):
            nc.scalar.activation(picked[:, t, :], planes[0][t][:].indirect(key_list[:]), ACT.Copy)
        grouped = [sb.tile([P, I, PACK], BF16, name=f"grouped{z}", align_bytes=64) for z in range(PASSES)]
        neg_bias = sb.tile([P, I], F32, name="neg_bias")
        prior = sb.tile([P, I], F32, name="prior")
        nc.scalar.activation(
            neg_bias[:].rearrange("p (n c) -> p n c", c=2),
            spread[:, 0:2, :].rearrange("p c n -> p n c"),
            ACT.Copy,
            scale=-TEMP,
        )
        nc.scalar.copy(prior[:].rearrange("p (n c) -> p n c", c=2), spread[:, 2:4, :].rearrange("p c n -> p n c"))

        for t in range(2):
            nc.scalar.activation(picked_late[:, t, :], planes[1][t][:].indirect(key_list[:]), ACT.Copy)

        picked_scales = sb.tile([P, PASSES, J], U8, name="picked_scales")
        tok_scales = sb.tile([P, PASSES, J], U8, name="tok_scales", align_bytes=64)
        tok_scales_i32 = tok_scales[:].rearrange("p z j -> p (z j)").bitcast(I32)
        picked_scales_i32 = picked_scales[:].rearrange("p z j -> p (z j)").bitcast(I32)
        nc.vector.memset(tok_scales_i32, 0)
        for z in range(PASSES):
            nc.vector.tensor_copy(picked_scales[:, z, :], scale_rows[:, z, :].indirect(tok_list[:]))
        for r in range(4):
            nc.scalar.dma_start(out=tok_scales_i32[r:P:32], in_=picked_scales_i32[8 * r : P : 32])

        key_codes = [sb.tile([P, I], U32, name=f"key_codes{z}", align_bytes=64) for z in range(PASSES)]
        key_scales = [sb.tile([P, I], U8, name=f"key_scales{z}", align_bytes=64) for z in range(PASSES)]
        tok_words = [
            [sb.tile([P, P], U16, name=f"tok_words{z}{h}", align_bytes=64) for h in range(HALVES)]
            for z in range(PASSES)
        ]
        acc = [ps.tile([P, I], F32, name=f"acc{h}") for h in range(HALVES)]

        def quantize(z, lo, hi):
            nc.vector.quantize_mx(
                out=key_codes[z][:, lo:hi].bitcast(E5M2),
                scales=key_scales[z][:, lo:hi],
                in_=grouped[z][:, lo:hi, :].rearrange("p i t -> p (i t)"),
            )

        def pick_words(z, h):
            nc.vector.tensor_copy(
                tok_words[z][h][:], words[z][:].indirect(tok_list[:, LIST_COLS * h : LIST_COLS * (h + 1)])
            )

        def multiply(z, h):
            nc.tensor.matmul_mx(
                out=acc[h][:],
                lhsT=tok_words[z][h][:].bitcast(E2M1),
                lhsT_scale=tok_scales[:, z, P * h : P * (h + 1)],
                rhs=key_codes[z][:].bitcast(E5M2),
                rhs_scale=key_scales[z][:],
                start=(z == 0),
                stop=(z == PASSES - 1),
            )

        pick_words(0, 0)
        pick_words(0, 1)
        nc.vector.tensor_copy(grouped[0][:], picked[:].rearrange("p t i -> p i t"))
        quantize(0, 0, I)
        for h in range(HALVES):
            multiply(0, h)

        nc.vector.tensor_copy(grouped[1][:, :, 0:2], picked_late[:].rearrange("p t i -> p i t"))
        nc.vector.tensor_copy(grouped[1][:, :, 2], planes[1][2][:].indirect(key_list[:]))
        picked_last = sb.tile([P, P], BF16, name="picked_last")
        nc.scalar.activation(picked_last[:], planes[1][3][:].indirect(key_list[:, LIST_COLS:]), ACT.Copy)
        nc.vector.tensor_copy(grouped[1][:, 0:P, 3], planes[1][3][:].indirect(key_list[:, 0:LIST_COLS]))
        nc.vector.tensor_copy(grouped[1][:, P:I, 3], picked_last[:])
        quantize(1, 0, P)
        pick_words(1, 0)
        quantize(1, P, I)
        multiply(1, 0)
        pick_words(1, 1)
        multiply(1, 1)

        neg = [sb.tile([P, I], F32, name=f"neg{h}") for h in range(HALVES)]
        low = [sb.tile([P, 1], F32, name=f"low{h}") for h in range(HALVES)]
        expo = [sb.tile([P, I], F32, name=f"expo{h}") for h in range(HALVES)]
        weighted = [sb.tile([P, I], F32, name=f"weighted{h}") for h in range(HALVES)]
        total = [sb.tile([P, 1], F32, name=f"total{h}") for h in range(HALVES)]
        raised = [sb.tile([P, I], F32, name=f"raised{h}") for h in range(HALVES)]
        factor = [sb.tile([P, 1], F32, name=f"factor{h}") for h in range(HALVES)]
        result = [sb.tile([P, I], F32, name=f"result{h}") for h in range(HALVES)]
        for h in range(HALVES):
            nc.vector.scalar_tensor_tensor(neg[h][:], acc[h][:], -TEMP, neg_bias[:], ALU.mult, ALU.add)
        for h in range(HALVES):
            nc.vector.tensor_reduce(low[h][:], neg[h][:], mybir.AxisListType.X, ALU.min)
            nc.scalar.activation(expo[h][:], neg[h][:], ACT.Exp, bias=low[h][:], scale=-1.0)
        for h in range(HALVES):
            nc.vector.scalar_tensor_tensor(
                weighted[h][:], expo[h][:], 1.0, prior[:], ALU.mult, ALU.mult, accum_out=total[h][:]
            )
        for h in range(HALVES):
            nc.scalar.activation(raised[h][:], weighted[h][:], ACT.Copy, scale=SHARE)
            nc.vector.reciprocal(factor[h][:], total[h][:])
        for h in range(HALVES):
            nc.vector.scalar_tensor_tensor(
                result[h][:], raised[h][:], factor[h][:], prior[:], ALU.mult, ALU.subtract
            )
            nc.sync.dma_start(out=out[P * h : P * (h + 1), :], in_=result[h][:])
